import numpy as np
import ml_dtypes


def mxq(x, axis, fmt="e4m3"):
    dtype, down = {"e4m3": (ml_dtypes.float8_e4m3fn, 7), "e5m2": (ml_dtypes.float8_e5m2, 14)}[fmt]
    v = np.moveaxis(np.asarray(x, np.float32).astype(ml_dtypes.bfloat16).astype(np.float64), axis, -1)
    blocks = v.reshape(v.shape[:-1] + (-1, 32))
    amax = np.abs(blocks).max(-1, keepdims=True)
    byte = np.maximum(np.where(amax > 0, np.frexp(amax)[1] - 1 + 127, 0) - down, 1)
    scale = np.exp2(byte - 127.0)
    codes = (blocks / scale).astype(np.float32).astype(dtype).astype(np.float64)
    return np.moveaxis((codes * scale).reshape(v.shape), -1, axis)


WIDE = False


def mx_kscale(k):
    if not WIDE:
        return np.ones(k)
    levels = np.array([10, -10, 5, -5, 0])
    if k % 512:
        return np.exp2(np.random.permutation(np.resize(levels, k // 32))).repeat(32)
    a = np.empty((k // 512, 16))
    for p in range(k // 512):
        a[p, :8] = np.random.permutation(np.resize(levels, 8))
        for g in range(8):
            far = levels[np.abs(levels - a[p, g]) >= 10]
            a[p, g + 8] = far[np.random.randint(len(far))]
    return np.exp2(a.ravel()).repeat(32)


def f64(x):
    return np.asarray(x).astype(np.float64)


def striped(idx):
    return np.tile(idx.reshape(-1, 16).T, (8, 1)).astype(np.uint16)


def unstriped(offs):
    return offs[:16].T.reshape(-1).astype(np.int64)


def pack_weight(w):
    k, n = w.shape
    w = f64(np.asarray(w, np.float32).astype(ml_dtypes.bfloat16)).reshape(k // 32, 32, n)
    amax = np.abs(w).max(1)
    byte = np.clip(np.where(amax > 0, np.frexp(amax)[1] - 1 + 127 - 7, 1), 1, 254)
    scaled = (w * np.exp2(127.0 - byte)[:, None, :]).reshape(k, n).astype(np.float32)
    words = np.ascontiguousarray(scaled.reshape(k // 512, 128, 4, n).transpose(0, 1, 3, 2)).astype(ml_dtypes.float8_e4m3fn).view(np.uint8)
    return words, np.ascontiguousarray(byte.astype(np.uint8).reshape(k // 512, 16, n))


def unpack_weight(words, scales):
    g, p, n, _ = words.shape
    vals = np.ascontiguousarray(words).view(ml_dtypes.float8_e4m3fn).astype(np.float64) * np.repeat(np.exp2(scales.astype(np.float64) - 127.0), 8, axis=1)[..., None]
    return vals.transpose(0, 1, 3, 2).reshape(g * 512, n)


def sigmoid(v):
    return 1.0 / (1.0 + np.exp(-np.maximum(v, -700.0)))


K, T, S, D, N = 512, 2048, 512, 8, 128


def setup_inputs():
    n = np.random.standard_normal
    s = mx_kscale(K)[:, None]
    packed_xT = pack_weight(n((K, T)) * s)
    return {
        "x_words": packed_xT[0],
        "x_scales": packed_xT[1],
        "w1": (n((K, N)) / np.sqrt(K) / s).astype(np.float32),
        "w2": (n((K, N)) / np.sqrt(K) / s).astype(np.float32),
        "offs": striped(np.random.permutation(T)[:S]),
    }


def reference(x_words, x_scales, w1, w2, offs):
    xq = unpack_weight(x_words, x_scales)[:, unstriped(offs)]
    ys = mxq(f64(w1), 0, "e4m3").T @ xq
    ls = np.log(sigmoid(ys) + 0.02)
    yu = mxq(f64(w2), 0, "e4m3").T @ xq
    iou = 0.9 * sigmoid(yu) + 0.05
    al = np.exp(0.5 * ls + 3.0 * np.log(iou))
    mi = iou.reshape(len(iou), -1, D).max(axis=2)
    mt = al.reshape(len(al), -1, D).max(axis=2) + 0.01
    return al * np.repeat(mi / mt, D, axis=1)

@@ -1,0 +1,126 @@
+from contextlib import ExitStack
+
+import concourse.mybir as mybir
+
+K, T, S, D, M = 512, 2048, 512, 8, 128
+FLOPS = 2 * 2 * K * M * S
+
+F32 = mybir.dt.float32
+BF16 = mybir.dt.bfloat16
+I32 = mybir.dt.int32
+U32 = mybir.dt.uint32
+U16 = mybir.dt.uint16
+U8 = mybir.dt.uint8
+FP8X4 = mybir.dt.float8_e4m3fn_x4
+ACT = mybir.ActivationFunctionType
+ALU = mybir.AluOpType
+AX = mybir.AxisListType
+
+P = 128
+PACK = 4
+PIECE = 128
+HALF = S // 2
+
+
+def tile_picked_ytal_tgt_p_kernel(tc, x_words, x_scales, w1, w2, offs, out):
+    nc = tc.nc
+    with ExitStack() as ctx:
+        sb = ctx.enter_context(tc.tile_pool(name="sb", bufs=1))
+        ps = ctx.enter_context(tc.psum_pool(name="ps", bufs=1))
+
+        offsets = sb.tile([P, S // 16], U16, name="offsets")
+        nc.sync.dma_start(offsets[:], offs)
+
+        raws = []
+        for name, w in (("wu", w2), ("ws", w1)):
+            raw = sb.tile([P, PACK, M], F32, name=name + "_raw")
+            nc.sync.dma_start(raw[:], w.rearrange("(p j) m -> p j m", j=PACK))
+            raws.append(raw)
+
+        scale_table = sb.tile([P, T], U8, name="scale_table", align_bytes=64)
+        nc.vector.memset(scale_table[:, : T // 2].bitcast(I32), 0)
+        nc.gpsimd.memset(scale_table[:, T // 2 :].bitcast(I32), 0)
+        for q in range(4):
+            nc.sync.dma_start(
+                scale_table[32 * q : 32 * q + 4, :].bitcast(I32),
+                x_scales[0, 4 * q : 4 * q + 4, :].bitcast(I32),
+            )
+
+        word_table = sb.tile([P, T], U32, name="word_table", align_bytes=64)
+        nc.sync.dma_start(word_table[:].bitcast(I32), x_words[0].rearrange("p n t -> p (n t)").bitcast(I32))
+
+        weights = []
+        for name, raw in zip(("wu", "ws"), raws):
+            grouped = sb.tile([P, M, PACK], BF16, name=name + "_grouped", align_bytes=64)
+            nc.scalar.activation(out=grouped[:], in_=raw[:].rearrange("p j m -> p m j"), func=ACT.Copy)
+            codes = sb.tile([P, M], U32, name=name + "_codes", align_bytes=64)
+            scales = sb.tile([P, M], U8, name=name + "_scales", align_bytes=64)
+            nc.vector.quantize_mx(
+                out=codes[:].bitcast(FP8X4), scales=scales[:], in_=grouped[:].rearrange("p m j -> p (m j)")
+            )
+            weights.append((codes, scales))
+
+        picked_scales = sb.tile([P, S], U8, name="picked_scales", align_bytes=64)
+        nc.vector.tensor_copy(picked_scales[:], scale_table[:].indirect(offsets[:]))
+
+        th = sb.tile([P, 2, S], F32, name="th")
+        iou2 = sb.tile([P, S], F32, name="iou2")
+        for c in range(S // PIECE):
+            cols = slice(c * PIECE, (c + 1) * PIECE)
+            picked = sb.tile([P, PIECE], U32, name="picked%d" % c, align_bytes=64)
+            nc.vector.tensor_copy(picked[:], word_table[:].indirect(offsets[:, c * PIECE // 16 : (c + 1) * PIECE // 16]))
+            acc = ps.tile([P, 2, PIECE], F32, name="acc%d" % c)
+            for i, (codes, scales) in enumerate(weights):
+                nc.tensor.matmul_mx(
+                    out=acc[:, i, :],
+                    lhsT=codes[:].bitcast(FP8X4),
+                    lhsT_scale=scales[:],
+                    rhs=picked[:].bitcast(FP8X4),
+                    rhs_scale=picked_scales[:, cols],
+                    start=True,
+                    stop=True,
+                )
+            nc.scalar.activation(out=th[:, :, cols], in_=acc[:], func=ACT.Tanh, scale=0.5)
+            nc.scalar.activation(out=iou2[:, cols], in_=th[:, 0, cols], func=ACT.Square, scale=0.45, bias=0.5)
+
+        tu = th[:, 0, :]
+        ts = th[:, 1, :]
+        cube = sb.tile([P, S], F32, name="cube")
+        part = sb.tile([P, S], F32, name="part")
+        z = sb.tile([P, S], F32, name="z")
+        tu_max = sb.tile([P, S // D], F32, name="tu_max")
+        z_max = sb.tile([P, S // D], F32, name="z_max")
+        halves = [slice(h * HALF, (h + 1) * HALF) for h in range(2)]
+        groups = [slice(h * HALF // D, (h + 1) * HALF // D) for h in range(2)]
+        for cols in halves:
+            nc.vector.scalar_tensor_tensor(cube[:, cols], tu[:, cols], 0.5 / 0.45, iou2[:, cols], ALU.add, ALU.mult)
+        for cols in halves:
+            nc.vector.scalar_tensor_tensor(part[:, cols], ts[:, cols], 1.04, cube[:, cols], ALU.add, ALU.mult)
+        for cols in halves:
+            nc.vector.tensor_tensor(z[:, cols], part[:, cols], cube[:, cols], ALU.mult)
+        for cols, g in zip(halves, groups):
+            nc.vector.tensor_reduce(z_max[:, g], z[:, cols].rearrange("p (v d) -> p v d", d=D), AX.X, ALU.max)
+        nc.vector.tensor_reduce(tu_max[:], tu.rearrange("p (v d) -> p v d", d=D), AX.X, ALU.max)
+
+        top = sb.tile([P, S // D], F32, name="top")
+        den = sb.tile([P, S // D], F32, name="den")
+        inv = sb.tile([P, S // D], F32, name="inv")
+        factor = sb.tile([P, S // D], F32, name="factor")
+        al = sb.tile([P, S], F32, name="al")
+        res = sb.tile([P, S], F32, name="res")
+        nc.scalar.activation(out=top[:], in_=z_max[:], func=ACT.Sqrt, scale=0.5)
+        nc.scalar.activation(out=den[:], in_=top[:], func=ACT.Identity, bias=0.01 / 0.45)
+        for cols in halves:
+            nc.scalar.activation(out=al[:, cols], in_=z[:, cols], func=ACT.Sqrt, scale=0.5 * 0.45 * 0.45)
+        for g in groups:
+            nc.vector.reciprocal(inv[:, g], den[:, g])
+        for g in groups:
+            nc.vector.scalar_tensor_tensor(factor[:, g], tu_max[:, g], 0.5 / 0.45, inv[:, g], ALU.add, ALU.mult)
+        for cols, g, queue in zip(halves, groups, (nc.sync, nc.scalar)):
+            nc.vector.tensor_tensor(
+                res[:, cols].rearrange("p (v d) -> p v d", d=D),
+                al[:, cols].rearrange("p (v d) -> p v d", d=D),
+                factor[:, g].unsqueeze(2).to_broadcast([P, HALF // D, D]),
+                ALU.mult,
+            )
+            queue.dma_start(out[:, cols], res[:, cols])

@@ -18,7 +18,6 @@ AX = mybir.AxisListType
 
 P = 128
 PACK = 4
-PIECE = 128
 HALF = S // 2
 
 
@@ -28,14 +27,27 @@ def tile_picked_ytal_tgt_p_kernel(tc, x_words, x_scales, w1, w2, offs, out):
         sb = ctx.enter_context(tc.tile_pool(name="sb", bufs=1))
         ps = ctx.enter_context(tc.psum_pool(name="ps", bufs=1))
 
-        offsets = sb.tile([P, S // 16], U16, name="offsets")
-        nc.sync.dma_start(offsets[:], offs)
-
-        raws = []
-        for name, w in (("wu", w2), ("ws", w1)):
+        def load_weight(name, w):
             raw = sb.tile([P, PACK, M], F32, name=name + "_raw")
             nc.sync.dma_start(raw[:], w.rearrange("(p j) m -> p j m", j=PACK))
-            raws.append(raw)
+            return raw
+
+        def quantise_weight(name, raw):
+            grouped = sb.tile([P, M, PACK], BF16, name=name + "_grouped", align_bytes=64)
+            nc.scalar.activation(out=grouped[:], in_=raw[:].rearrange("p j m -> p m j"), func=ACT.Copy)
+            codes = sb.tile([P, M], U32, name=name + "_codes", align_bytes=64)
+            scales = sb.tile([P, M], U8, name=name + "_scales", align_bytes=64)
+            nc.vector.quantize_mx(
+                out=codes[:].bitcast(FP8X4), scales=scales[:], in_=grouped[:].rearrange("p m j -> p (m j)")
+            )
+            return codes, scales
+
+        def group_max(dst, src):
+            nc.vector.tensor_reduce(dst, src.rearrange("p (v d) -> p v d", d=D), AX.X, ALU.max)
+
+        offsets = sb.tile([P, S // 16], U16, name="offsets")
+        w2_raw = load_weight("w2", w2)
+        nc.sync.dma_start(offsets[:], offs)
 
         scale_table = sb.tile([P, T], U8, name="scale_table", align_bytes=64)
         nc.vector.memset(scale_table[:, : T // 2].bitcast(I32), 0)
@@ -48,68 +60,70 @@ def tile_picked_ytal_tgt_p_kernel(tc, x_words, x_scales, w1, w2, offs, out):
 
         word_table = sb.tile([P, T], U32, name="word_table", align_bytes=64)
         nc.sync.dma_start(word_table[:].bitcast(I32), x_words[0].rearrange("p n t -> p (n t)").bitcast(I32))
+        w1_raw = load_weight("w1", w1)
 
-        weights = []
-        for name, raw in zip(("wu", "ws"), raws):
-            grouped = sb.tile([P, M, PACK], BF16, name=name + "_grouped", align_bytes=64)
-            nc.scalar.activation(out=grouped[:], in_=raw[:].rearrange("p j m -> p m j"), func=ACT.Copy)
-            codes = sb.tile([P, M], U32, name=name + "_codes", align_bytes=64)
-            scales = sb.tile([P, M], U8, name=name + "_scales", align_bytes=64)
-            nc.vector.quantize_mx(
-                out=codes[:].bitcast(FP8X4), scales=scales[:], in_=grouped[:].rearrange("p m j -> p (m j)")
-            )
-            weights.append((codes, scales))
+        w2_mx = quantise_weight("w2", w2_raw)
 
         picked_scales = sb.tile([P, S], U8, name="picked_scales", align_bytes=64)
         nc.vector.tensor_copy(picked_scales[:], scale_table[:].indirect(offsets[:]))
 
-        th = sb.tile([P, 2, S], F32, name="th")
-        iou2 = sb.tile([P, S], F32, name="iou2")
-        for c in range(S // PIECE):
-            cols = slice(c * PIECE, (c + 1) * PIECE)
-            picked = sb.tile([P, PIECE], U32, name="picked%d" % c, align_bytes=64)
-            nc.vector.tensor_copy(picked[:], word_table[:].indirect(offsets[:, c * PIECE // 16 : (c + 1) * PIECE // 16]))
-            acc = ps.tile([P, 2, PIECE], F32, name="acc%d" % c)
-            for i, (codes, scales) in enumerate(weights):
-                nc.tensor.matmul_mx(
-                    out=acc[:, i, :],
-                    lhsT=codes[:].bitcast(FP8X4),
-                    lhsT_scale=scales[:],
-                    rhs=picked[:].bitcast(FP8X4),
-                    rhs_scale=picked_scales[:, cols],
-                    start=True,
-                    stop=True,
-                )
-            nc.scalar.activation(out=th[:, :, cols], in_=acc[:], func=ACT.Tanh, scale=0.5)
-            nc.scalar.activation(out=iou2[:, cols], in_=th[:, 0, cols], func=ACT.Square, scale=0.45, bias=0.5)
+        halves = [slice(h * HALF, (h + 1) * HALF) for h in range(2)]
+        groups = [slice(h * HALF // D, (h + 1) * HALF // D) for h in range(2)]
 
-        tu = th[:, 0, :]
-        ts = th[:, 1, :]
+        picked = []
+        for h in range(2):
+            words = sb.tile([P, HALF], U32, name="picked%d" % h, align_bytes=64)
+            nc.vector.tensor_copy(words[:], word_table[:].indirect(offsets[:, h * HALF // 16 : (h + 1) * HALF // 16]))
+            picked.append(words)
+
+        w1_mx = quantise_weight("w1", w1_raw)
+
+        def product_tanh(name, weight, h, dst):
+            acc = ps.tile([P, HALF], F32, name="%s_acc%d" % (name, h))
+            nc.tensor.matmul_mx(
+                out=acc[:],
+                lhsT=weight[0][:].bitcast(FP8X4),
+                lhsT_scale=weight[1][:],
+                rhs=picked[h][:].bitcast(FP8X4),
+                rhs_scale=picked_scales[:, halves[h]],
+                start=True,
+                stop=True,
+            )
+            nc.scalar.activation(out=dst[:, halves[h]], in_=acc[:], func=ACT.Tanh, scale=0.5)
+
+        tu = sb.tile([P, S], F32, name="tu")
+        ts = sb.tile([P, S], F32, name="ts")
+        iou2 = sb.tile([P, S], F32, name="iou2")
+        for h, cols in enumerate(halves):
+            product_tanh("u", w2_mx, h, tu)
+            nc.scalar.activation(out=iou2[:, cols], in_=tu[:, cols], func=ACT.Square, scale=0.45, bias=0.5)
+        for h in range(2):
+            product_tanh("s", w1_mx, h, ts)
+
         cube = sb.tile([P, S], F32, name="cube")
-        part = sb.tile([P, S], F32, name="part")
+        sixth = sb.tile([P, S], F32, name="sixth")
         z = sb.tile([P, S], F32, name="z")
         tu_max = sb.tile([P, S // D], F32, name="tu_max")
         z_max = sb.tile([P, S // D], F32, name="z_max")
-        halves = [slice(h * HALF, (h + 1) * HALF) for h in range(2)]
-        groups = [slice(h * HALF // D, (h + 1) * HALF // D) for h in range(2)]
+        group_max(tu_max[:, groups[0]], tu[:, halves[0]])
         for cols in halves:
             nc.vector.scalar_tensor_tensor(cube[:, cols], tu[:, cols], 0.5 / 0.45, iou2[:, cols], ALU.add, ALU.mult)
+            nc.vector.tensor_tensor(sixth[:, cols], cube[:, cols], cube[:, cols], ALU.mult)
         for cols in halves:
-            nc.vector.scalar_tensor_tensor(part[:, cols], ts[:, cols], 1.04, cube[:, cols], ALU.add, ALU.mult)
-        for cols in halves:
-            nc.vector.tensor_tensor(z[:, cols], part[:, cols], cube[:, cols], ALU.mult)
+            nc.vector.scalar_tensor_tensor(z[:, cols], ts[:, cols], 1.04, sixth[:, cols], ALU.add, ALU.mult)
         for cols, g in zip(halves, groups):
-            nc.vector.tensor_reduce(z_max[:, g], z[:, cols].rearrange("p (v d) -> p v d", d=D), AX.X, ALU.max)
-        nc.vector.tensor_reduce(tu_max[:], tu.rearrange("p (v d) -> p v d", d=D), AX.X, ALU.max)
+            group_max(z_max[:, g], z[:, cols])
+        group_max(tu_max[:, groups[1]], tu[:, halves[1]])
 
-        top = sb.tile([P, S // D], F32, name="top")
         den = sb.tile([P, S // D], F32, name="den")
         inv = sb.tile([P, S // D], F32, name="inv")
         factor = sb.tile([P, S // D], F32, name="factor")
         al = sb.tile([P, S], F32, name="al")
         res = sb.tile([P, S], F32, name="res")
-        nc.scalar.activation(out=top[:], in_=z_max[:], func=ACT.Sqrt, scale=0.5)
-        nc.scalar.activation(out=den[:], in_=top[:], func=ACT.Identity, bias=0.01 / 0.45)
+        for cols, g in zip(halves, groups):
+            top = al[:, cols.start : cols.start + HALF // D]
+            nc.scalar.activation(out=top, in_=z_max[:, g], func=ACT.Sqrt, scale=0.5)
+            nc.scalar.activation(out=den[:, g], in_=top, func=ACT.Identity, bias=0.01 / 0.45)
         for cols in halves:
             nc.scalar.activation(out=al[:, cols], in_=z[:, cols], func=ACT.Sqrt, scale=0.5 * 0.45 * 0.45)
         for g in groups:

@@ -19,6 +19,8 @@ AX = mybir.AxisListType
 P = 128
 PACK = 4
 HALF = S // 2
+EARLY = 512
+PIECE = 128
 
 
 def tile_picked_ytal_tgt_p_kernel(tc, x_words, x_scales, w1, w2, offs, out):
@@ -32,9 +34,12 @@ def tile_picked_ytal_tgt_p_kernel(tc, x_words, x_scales, w1, w2, offs, out):
             nc.sync.dma_start(raw[:], w.rearrange("(p j) m -> p j m", j=PACK))
             return raw
 
-        def quantise_weight(name, raw):
+        def quantise_weight(name, raw, split):
             grouped = sb.tile([P, M, PACK], BF16, name=name + "_grouped", align_bytes=64)
-            nc.scalar.activation(out=grouped[:], in_=raw[:].rearrange("p j m -> p m j"), func=ACT.Copy)
+            turned = raw[:].rearrange("p j m -> p m j")
+            nc.scalar.activation(out=grouped[:, :split, :], in_=turned[:, :split, :], func=ACT.Copy)
+            if split < M:
+                nc.vector.tensor_copy(grouped[:, split:, :], turned[:, split:, :])
             codes = sb.tile([P, M], U32, name=name + "_codes", align_bytes=64)
             scales = sb.tile([P, M], U8, name=name + "_scales", align_bytes=64)
             nc.vector.quantize_mx(
@@ -49,20 +54,23 @@ def tile_picked_ytal_tgt_p_kernel(tc, x_words, x_scales, w1, w2, offs, out):
         w2_raw = load_weight("w2", w2)
         nc.sync.dma_start(offsets[:], offs)
 
+        word_table = sb.tile([P, T], U32, name="word_table", align_bytes=64)
+        words_hbm = x_words[0].rearrange("p n t -> p (n t)").bitcast(I32)
+        nc.sync.dma_start(word_table[:, :EARLY].bitcast(I32), words_hbm[:, :EARLY])
+
         scale_table = sb.tile([P, T], U8, name="scale_table", align_bytes=64)
         nc.vector.memset(scale_table[:, : T // 2].bitcast(I32), 0)
         nc.gpsimd.memset(scale_table[:, T // 2 :].bitcast(I32), 0)
-        for q in range(4):
+        for r in range(4):
             nc.sync.dma_start(
-                scale_table[32 * q : 32 * q + 4, :].bitcast(I32),
-                x_scales[0, 4 * q : 4 * q + 4, :].bitcast(I32),
+                scale_table[r:P:32, :].bitcast(I32),
+                x_scales[0, r:16:4, :].bitcast(I32),
             )
 
-        word_table = sb.tile([P, T], U32, name="word_table", align_bytes=64)
-        nc.sync.dma_start(word_table[:].bitcast(I32), x_words[0].rearrange("p n t -> p (n t)").bitcast(I32))
+        nc.sync.dma_start(word_table[:, EARLY:].bitcast(I32), words_hbm[:, EARLY:])
         w1_raw = load_weight("w1", w1)
 
-        w2_mx = quantise_weight("w2", w2_raw)
+        w2_mx = quantise_weight("w2", w2_raw, M)
 
         picked_scales = sb.tile([P, S], U8, name="picked_scales", align_bytes=64)
         nc.vector.tensor_copy(picked_scales[:], scale_table[:].indirect(offsets[:]))
@@ -73,32 +81,38 @@ def tile_picked_ytal_tgt_p_kernel(tc, x_words, x_scales, w1, w2, offs, out):
         picked = []
         for h in range(2):
             words = sb.tile([P, HALF], U32, name="picked%d" % h, align_bytes=64)
-            nc.vector.tensor_copy(words[:], word_table[:].indirect(offsets[:, h * HALF // 16 : (h + 1) * HALF // 16]))
+            for c in range(0, HALF, PIECE):
+                first = (h * HALF + c) // 16
+                nc.vector.tensor_copy(
+                    words[:, c : c + PIECE], word_table[:].indirect(offsets[:, first : first + PIECE // 16])
+                )
             picked.append(words)
 
-        w1_mx = quantise_weight("w1", w1_raw)
+        w1_mx = quantise_weight("w1", w1_raw, M // 2)
 
-        def product_tanh(name, weight, h, dst):
-            acc = ps.tile([P, HALF], F32, name="%s_acc%d" % (name, h))
+        def product_tanh(name, weight, start, width, dst):
+            cols = slice(start, start + width)
+            acc = ps.tile([P, width], F32, name="%s_acc%d" % (name, start))
             nc.tensor.matmul_mx(
                 out=acc[:],
                 lhsT=weight[0][:].bitcast(FP8X4),
                 lhsT_scale=weight[1][:],
-                rhs=picked[h][:].bitcast(FP8X4),
-                rhs_scale=picked_scales[:, halves[h]],
+                rhs=picked[start // HALF][:, start % HALF : start % HALF + width].bitcast(FP8X4),
+                rhs_scale=picked_scales[:, cols],
                 start=True,
                 stop=True,
             )
-            nc.scalar.activation(out=dst[:, halves[h]], in_=acc[:], func=ACT.Tanh, scale=0.5)
+            nc.scalar.activation(out=dst[:, cols], in_=acc[:], func=ACT.Tanh, scale=0.5)
 
         tu = sb.tile([P, S], F32, name="tu")
         ts = sb.tile([P, S], F32, name="ts")
         iou2 = sb.tile([P, S], F32, name="iou2")
-        for h, cols in enumerate(halves):
-            product_tanh("u", w2_mx, h, tu)
+        for start in range(0, S, PIECE):
+            cols = slice(start, start + PIECE)
+            product_tanh("u", w2_mx, start, PIECE, tu)
             nc.scalar.activation(out=iou2[:, cols], in_=tu[:, cols], func=ACT.Square, scale=0.45, bias=0.5)
-        for h in range(2):
-            product_tanh("s", w1_mx, h, ts)
+        for start in range(0, S, HALF):
+            product_tanh("s", w1_mx, start, HALF, ts)
 
         cube = sb.tile([P, S], F32, name="cube")
         sixth = sb.tile([P, S], F32, name="sixth")

from contextlib import ExitStack

import concourse.mybir as mybir

K, T, S, D, M = 512, 2048, 512, 8, 128
FLOPS = 2 * 2 * K * M * S

F32 = mybir.dt.float32
BF16 = mybir.dt.bfloat16
I32 = mybir.dt.int32
U32 = mybir.dt.uint32
U16 = mybir.dt.uint16
U8 = mybir.dt.uint8
FP8X4 = mybir.dt.float8_e4m3fn_x4
ACT = mybir.ActivationFunctionType
ALU = mybir.AluOpType
AX = mybir.AxisListType

P = 128
PACK = 4
HALF = S // 2
EARLY = 512
PIECE = 128


def tile_picked_ytal_tgt_p_kernel(tc, x_words, x_scales, w1, w2, offs, out):
    nc = tc.nc
    with ExitStack() as ctx:
        sb = ctx.enter_context(tc.tile_pool(name="sb", bufs=1))
        ps = ctx.enter_context(tc.psum_pool(name="ps", bufs=1))

        def load_weight(name, w):
            raw = sb.tile([P, PACK, M], F32, name=name + "_raw")
            nc.sync.dma_start(raw[:], w.rearrange("(p j) m -> p j m", j=PACK))
            return raw

        def quantise_weight(name, raw, split):
            grouped = sb.tile([P, M, PACK], BF16, name=name + "_grouped", align_bytes=64)
            turned = raw[:].rearrange("p j m -> p m j")
            nc.scalar.activation(out=grouped[:, :split, :], in_=turned[:, :split, :], func=ACT.Copy)
            if split < M:
                nc.vector.tensor_copy(grouped[:, split:, :], turned[:, split:, :])
            codes = sb.tile([P, M], U32, name=name + "_codes", align_bytes=64)
            scales = sb.tile([P, M], U8, name=name + "_scales", align_bytes=64)
            nc.vector.quantize_mx(
                out=codes[:].bitcast(FP8X4), scales=scales[:], in_=grouped[:].rearrange("p m j -> p (m j)")
            )
            return codes, scales

        def group_max(dst, src):
            nc.vector.tensor_reduce(dst, src.rearrange("p (v d) -> p v d", d=D), AX.X, ALU.max)

        offsets = sb.tile([P, S // 16], U16, name="offsets")
        w2_raw = load_weight("w2", w2)
        nc.sync.dma_start(offsets[:], offs)

        word_table = sb.tile([P, T], U32, name="word_table", align_bytes=64)
        words_hbm = x_words[0].rearrange("p n t -> p (n t)").bitcast(I32)
        nc.sync.dma_start(word_table[:, :EARLY].bitcast(I32), words_hbm[:, :EARLY])

        scale_table = sb.tile([P, T], U8, name="scale_table", align_bytes=64)
        nc.vector.memset(scale_table[:, : T // 2].bitcast(I32), 0)
        nc.gpsimd.memset(scale_table[:, T // 2 :].bitcast(I32), 0)
        for r in range(4):
            nc.sync.dma_start(
                scale_table[r:P:32, :].bitcast(I32),
                x_scales[0, r:16:4, :].bitcast(I32),
            )

        nc.sync.dma_start(word_table[:, EARLY:].bitcast(I32), words_hbm[:, EARLY:])
        w1_raw = load_weight("w1", w1)

        w2_mx = quantise_weight("w2", w2_raw, M)

        picked_scales = sb.tile([P, S], U8, name="picked_scales", align_bytes=64)
        nc.vector.tensor_copy(picked_scales[:], scale_table[:].indirect(offsets[:]))

        halves = [slice(h * HALF, (h + 1) * HALF) for h in range(2)]
        groups = [slice(h * HALF // D, (h + 1) * HALF // D) for h in range(2)]

        picked = []
        for h in range(2):
            words = sb.tile([P, HALF], U32, name="picked%d" % h, align_bytes=64)
            for c in range(0, HALF, PIECE):
                first = (h * HALF + c) // 16
                nc.vector.tensor_copy(
                    words[:, c : c + PIECE], word_table[:].indirect(offsets[:, first : first + PIECE // 16])
                )
            picked.append(words)

        w1_mx = quantise_weight("w1", w1_raw, M // 2)

        def product_tanh(name, weight, start, width, dst):
            cols = slice(start, start + width)
            acc = ps.tile([P, width], F32, name="%s_acc%d" % (name, start))
            nc.tensor.matmul_mx(
                out=acc[:],
                lhsT=weight[0][:].bitcast(FP8X4),
                lhsT_scale=weight[1][:],
                rhs=picked[start // HALF][:, start % HALF : start % HALF + width].bitcast(FP8X4),
                rhs_scale=picked_scales[:, cols],
                start=True,
                stop=True,
            )
            nc.scalar.activation(out=dst[:, cols], in_=acc[:], func=ACT.Tanh, scale=0.5)

        tu = sb.tile([P, S], F32, name="tu")
        ts = sb.tile([P, S], F32, name="ts")
        iou2 = sb.tile([P, S], F32, name="iou2")
        for start in range(0, S, PIECE):
            cols = slice(start, start + PIECE)
            product_tanh("u", w2_mx, start, PIECE, tu)
            nc.scalar.activation(out=iou2[:, cols], in_=tu[:, cols], func=ACT.Square, scale=0.45, bias=0.5)
        for start in range(0, S, HALF):
            product_tanh("s", w1_mx, start, HALF, ts)

        cube = sb.tile([P, S], F32, name="cube")
        sixth = sb.tile([P, S], F32, name="sixth")
        z = sb.tile([P, S], F32, name="z")
        tu_max = sb.tile([P, S // D], F32, name="tu_max")
        z_max = sb.tile([P, S // D], F32, name="z_max")
        group_max(tu_max[:, groups[0]], tu[:, halves[0]])
        for cols in halves:
            nc.vector.scalar_tensor_tensor(cube[:, cols], tu[:, cols], 0.5 / 0.45, iou2[:, cols], ALU.add, ALU.mult)
            nc.vector.tensor_tensor(sixth[:, cols], cube[:, cols], cube[:, cols], ALU.mult)
        for cols in halves:
            nc.vector.scalar_tensor_tensor(z[:, cols], ts[:, cols], 1.04, sixth[:, cols], ALU.add, ALU.mult)
        for cols, g in zip(halves, groups):
            group_max(z_max[:, g], z[:, cols])
        group_max(tu_max[:, groups[1]], tu[:, halves[1]])

        den = sb.tile([P, S // D], F32, name="den")
        inv = sb.tile([P, S // D], F32, name="inv")
        factor = sb.tile([P, S // D], F32, name="factor")
        al = sb.tile([P, S], F32, name="al")
        res = sb.tile([P, S], F32, name="res")
        for cols, g in zip(halves, groups):
            top = al[:, cols.start : cols.start + HALF // D]
            nc.scalar.activation(out=top, in_=z_max[:, g], func=ACT.Sqrt, scale=0.5)
            nc.scalar.activation(out=den[:, g], in_=top, func=ACT.Identity, bias=0.01 / 0.45)
        for cols in halves:
            nc.scalar.activation(out=al[:, cols], in_=z[:, cols], func=ACT.Sqrt, scale=0.5 * 0.45 * 0.45)
        for g in groups:
            nc.vector.reciprocal(inv[:, g], den[:, g])
        for g in groups:
            nc.vector.scalar_tensor_tensor(factor[:, g], tu_max[:, g], 0.5 / 0.45, inv[:, g], ALU.add, ALU.mult)
        for cols, g, queue in zip(halves, groups, (nc.sync, nc.scalar)):
            nc.vector.tensor_tensor(
                res[:, cols].rearrange("p (v d) -> p v d", d=D),
                al[:, cols].rearrange("p (v d) -> p v d", d=D),
                factor[:, g].unsqueeze(2).to_broadcast([P, HALF // D, D]),
                ALU.mult,
            )
            queue.dma_start(out[:, cols], res[:, cols])
